import numpy as np
import ml_dtypes


def mxq(x, axis, fmt="e4m3"):
    dtype, down = {"e4m3": (ml_dtypes.float8_e4m3fn, 7), "e5m2": (ml_dtypes.float8_e5m2, 14)}[fmt]
    v = np.moveaxis(np.asarray(x, np.float32).astype(ml_dtypes.bfloat16).astype(np.float64), axis, -1)
    blocks = v.reshape(v.shape[:-1] + (-1, 32))
    amax = np.abs(blocks).max(-1, keepdims=True)
    byte = np.maximum(np.where(amax > 0, np.frexp(amax)[1] - 1 + 127, 0) - down, 1)
    scale = np.exp2(byte - 127.0)
    codes = (blocks / scale).astype(np.float32).astype(dtype).astype(np.float64)
    return np.moveaxis((codes * scale).reshape(v.shape), -1, axis)


WIDE = False


def mx_kscale(k):
    if not WIDE:
        return np.ones(k)
    levels = np.array([10, -10, 5, -5, 0])
    if k % 512:
        return np.exp2(np.random.permutation(np.resize(levels, k // 32))).repeat(32)
    a = np.empty((k // 512, 16))
    for p in range(k // 512):
        a[p, :8] = np.random.permutation(np.resize(levels, 8))
        for g in range(8):
            far = levels[np.abs(levels - a[p, g]) >= 10]
            a[p, g + 8] = far[np.random.randint(len(far))]
    return np.exp2(a.ravel()).repeat(32)


def f64(x):
    return np.asarray(x).astype(np.float64)


def striped(idx):
    return np.tile(idx.reshape(-1, 16).T, (8, 1)).astype(np.uint16)


def unstriped(offs):
    return offs[:16].T.reshape(-1).astype(np.int64)


E2M1 = np.array([0.0, 0.5, 1.0, 1.5, 2.0, 3.0, 4.0, 6.0, -0.0, -0.5, -1.0, -1.5, -2.0, -3.0, -4.0, -6.0])


def pack_weight(w, fmt):
    k, n = w.shape
    w = f64(np.asarray(w, np.float32).astype(ml_dtypes.bfloat16)).reshape(k // 32, 32, n)
    amax = np.abs(w).max(1)
    if fmt == "e4m3":
        byte = np.frexp(amax)[1] - 1 + 127 - 7
    else:
        mant, ex = np.frexp(amax / 6.0)
        byte = np.where(mant > 0.5, ex, ex - 1) + 127
    byte = np.clip(np.where(amax > 0, byte, 1), 1, 254)
    scaled = (w * np.exp2(127.0 - byte)[:, None, :]).reshape(k, n).astype(np.float32)
    by_word = np.ascontiguousarray(scaled.reshape(k // 512, 128, 4, n).transpose(0, 1, 3, 2))
    if fmt == "e4m3":
        words = by_word.astype(ml_dtypes.float8_e4m3fn).view(np.uint8)
    else:
        c = by_word.astype(ml_dtypes.float4_e2m1fn).view(np.uint8) & 0xF
        words = (c[..., 0::2] | (c[..., 1::2] << 4)).reshape(k // 512, 128, 2 * n)
    return np.ascontiguousarray(words), np.ascontiguousarray(byte.astype(np.uint8).reshape(k // 512, 16, n))


def unpack_weight(words, scales, fmt):
    g, _, n = scales.shape
    words = np.ascontiguousarray(words).reshape(g, 128, n, -1)
    if fmt == "e4m3":
        vals = words.view(ml_dtypes.float8_e4m3fn).astype(np.float64)
    else:
        nib = np.empty((g, 128, n, 4), np.uint8)
        nib[..., 0::2] = words & 0xF
        nib[..., 1::2] = words >> 4
        vals = E2M1[nib]
    vals = vals * np.repeat(np.exp2(scales.astype(np.float64) - 127.0), 8, axis=1)[..., None]
    return vals.transpose(0, 1, 3, 2).reshape(g * 512, n)


def gelu(v):
    return 0.5 * v * (1.0 + np.tanh(np.sqrt(2.0 / np.pi) * (v + 0.044715 * v**3)))


def bf(x):
    return np.asarray(x, np.float32).astype(ml_dtypes.bfloat16)


def planes(Y):
    n, m = Y.shape
    b = f64(bf(Y)).reshape(n // 32, 32, m)
    amax = np.abs(b).max(1)
    byte = np.clip(np.where(amax > 0, np.frexp(amax)[1] - 1 + 127 - 7, 1), 1, 254)
    codes = (b * np.exp2(127.0 - byte)[:, None, :]).reshape(n, m).astype(np.float32).astype(ml_dtypes.float8_e4m3fn).view(np.uint8)
    words = codes.reshape(n // 512, 128, 4, m).transpose(0, 1, 3, 2)
    return np.ascontiguousarray(words), np.ascontiguousarray(byte.astype(np.uint8).reshape(n // 512, 16, m))


K, T, S, P, P2, H, N = 1024, 4096, 2048, 1024, 512, 512, 1024

def setup_inputs():
    n = np.random.standard_normal
    s = mx_kscale(K)[:, None]
    u = mx_kscale(H)[:, None]
    tab_words, tab_scales = pack_weight(n((K, T)) * s, "e4m3")
    w1 = (0.55 * n((K, H)) / np.sqrt(K) / s).astype(np.float32)
    w2_words, w2_scales = pack_weight(1.3 * n((K, H)) / np.sqrt(K) / s, "e2m1")
    gain = (2.0 * np.exp(0.3 * n(H)) * u[:, 0]).astype(np.float32)
    w3 = (n((H, N)) * np.exp(0.8 * n(N))[None, :] / np.sqrt(H) / u).astype(np.float32)
    return {"tab_words": tab_words, "tab_scales": tab_scales,
            "offs": striped(np.random.permutation(T)[:S]),
            "w1": w1, "w2_words": w2_words, "w2_scales": w2_scales,
            "gain": gain,
            "pos1": striped(np.random.permutation(S)[:P]),
            "pos2": striped(np.random.permutation(S)[:P]),
            "pos3": striped(np.random.permutation(P)[:P2]),
            "pos4": striped(np.random.permutation(S)[:P2]),
            "w3": w3}

def reference(tab_words, tab_scales, offs, w1, w2_words, w2_scales, gain, pos1, pos2, pos3, pos4, w3):
    v = unpack_weight(tab_words, tab_scales, "e4m3")[:, unstriped(offs)]
    w1q = mxq(f64(w1), 0, "e4m3")
    w2 = unpack_weight(w2_words, w2_scales, "e2m1")
    e1 = w1q.T @ v
    e2 = w2.T @ v
    h = f64(gain)[:, None] * (np.sin(e1) * np.tanh(e2))
    a1 = h[:, unstriped(pos1)] - h[:, unstriped(pos2)]
    a2 = np.maximum(a1[:, unstriped(pos3)], h[:, unstriped(pos4)])
    a2q = mxq(a2, 0, "e4m3")
    w3q = mxq(f64(w3), 0, "e4m3")
    y = w3q.T @ a2q
    words, scales = planes(y)
    return y, words, scales

@@ -1,0 +1,300 @@
+import math
+from contextlib import ExitStack
+
+import concourse.mybir as mybir
+
+K, T, S, PAIRS, KEPT, H, N = 1024, 4096, 2048, 1024, 512, 512, 1024
+FLOPS = 2 * K * H * S * 2 + 2 * H * N * KEPT
+
+F32 = mybir.dt.float32
+BF16 = mybir.dt.bfloat16
+I32 = mybir.dt.int32
+U32 = mybir.dt.uint32
+U16 = mybir.dt.uint16
+U8 = mybir.dt.uint8
+FP8X4 = mybir.dt.float8_e4m3fn_x4
+FP4X4 = mybir.dt.float4_e2m1fn_x4
+ALU = mybir.AluOpType
+ACT = mybir.ActivationFunctionType
+
+P = 128
+PACK = 4
+PASSES = K // (P * PACK)
+GROUPS = N // (P * PACK)
+BANK = 512
+PER_COL = 16
+OUT_COLS = 128
+HALF = 256
+DEPTH = 4
+LAG = 2
+
+
+def tile_list_letter_stylometry_traits_kernel(
+    tc, tab_words, tab_scales, offs, w1, w2_words, w2_scales, gain, pos1, pos2, pos3, pos4, w3, out_0, out_1, out_2
+):
+    nc = tc.nc
+    with ExitStack() as ctx:
+        lists = ctx.enter_context(tc.tile_pool(name="lists", bufs=1))
+        keep = ctx.enter_context(tc.tile_pool(name="keep", bufs=1))
+        ring = ctx.enter_context(tc.tile_pool(name="ring", bufs=2))
+        psum = ctx.enter_context(tc.psum_pool(name="psum", bufs=8))
+
+        def load_list(src, name):
+            tile = lists.tile(list(src.shape), U16, name=name)
+            nc.sync.dma_start(tile[:], src)
+            return tile
+
+        scale_rows = keep.tile([P, T], U8, name="scale_rows", align_bytes=64)
+        nc.vector.memset(scale_rows[32:64, :].bitcast(I32), 0)
+        nc.vector.memset(scale_rows[64:128, :].bitcast(I32), 0)
+        w2_planes_raw = keep.tile([P, PASSES * H], U8, name="w2_planes_raw", align_bytes=64)
+        nc.gpsimd.memset(w2_planes_raw[:].bitcast(I32), 0)
+        v_planes = [keep.tile([P, S], U8, name=f"v_plane{a}", align_bytes=64) for a in range(PASSES)]
+        for a in range(PASSES):
+            nc.gpsimd.memset(v_planes[a][:].bitcast(I32), 0)
+
+        offs_sb = load_list(offs, "offs_sb")
+        nc.sync.dma_start(scale_rows[0:32, :].bitcast(I32), tab_scales.rearrange("a q t -> (a q) t").bitcast(I32))
+        tab = [keep.tile([P, T], U32, name=f"tab{a}", tag=f"big{a}", align_bytes=64) for a in range(PASSES)]
+
+        def load_tab(a):
+            nc.sync.dma_start(tab[a][:].bitcast(I32), tab_words[a].rearrange("p t i -> p (t i)").bitcast(I32))
+
+        load_tab(0)
+        w2_raw = keep.tile([P, PASSES, 2 * H], U8, name="w2_raw")
+        nc.sync.dma_start(w2_raw[:].bitcast(I32), w2_words.rearrange("a p c -> p a c").bitcast(I32))
+        for q in range(4):
+            nc.gpsimd.dma_start(
+                w2_planes_raw[32 * q : 32 * q + 4, :].rearrange("r (a c) -> r a c", a=PASSES).bitcast(I32),
+                w2_scales[:, 4 * q : 4 * q + 4, :].rearrange("a r c -> r a c").bitcast(I32),
+            )
+        gain_sb = keep.tile([P, PACK], F32, name="gain_sb")
+        nc.sync.dma_start(gain_sb[:], gain.rearrange("(p t) -> p t", t=PACK))
+        pos1_sb = load_list(pos1, "pos1_sb")
+        pos2_sb = load_list(pos2, "pos2_sb")
+        pos3_sb = load_list(pos3, "pos3_sb")
+        w1_raw = [keep.tile([P, PACK, H], F32, name=f"w1_raw{a}", tag=f"raw{a}") for a in range(PASSES)]
+        for a in range(PASSES):
+            nc.sync.dma_start(w1_raw[a][:], w1[a * 512 : (a + 1) * 512, :].rearrange("(p j) c -> p j c", j=PACK))
+        load_tab(1)
+        pos4_sb = load_list(pos4, "pos4_sb")
+
+        def offsets(tile, first, count):
+            return tile[:, first // PER_COL : (first + count) // PER_COL]
+
+        picked_rows = keep.tile([P, S], U8, name="picked_rows", align_bytes=64)
+        nc.vector.tensor_copy(picked_rows[:], scale_rows[:].indirect(offs_sb[:]))
+        for a, queue in enumerate((nc.gpsimd, nc.scalar)):
+            for q in range(4):
+                row = 16 * a + 4 * q
+                queue.dma_start(
+                    v_planes[a][32 * q : 32 * q + 4, :].bitcast(I32), picked_rows[row : row + 4, :].bitcast(I32)
+                )
+        v_words = [keep.tile([P, S], U32, name="v_words0", align_bytes=64)]
+        nc.vector.tensor_copy(v_words[0][:], tab[0][:].indirect(offs_sb[:]))
+
+        def round_and_deal(dealt, raw):
+            nc.scalar.copy(
+                dealt.rearrange("p (t m j) -> p m t j", t=PACK, j=PACK),
+                raw.rearrange("p j (m t) -> p m t j", t=PACK),
+            )
+
+        def quantise(rounded, name):
+            codes = keep.tile([P, 512], U32, name=name + "_codes", align_bytes=64)
+            plane = keep.tile([P, 512], U8, name=name + "_plane", align_bytes=64)
+            nc.vector.quantize_mx(out=codes[:].bitcast(FP8X4), scales=plane[:], in_=rounded)
+            return codes, plane
+
+        w2_codes = keep.tile([P, PASSES * 2 * H], U8, name="w2_codes", align_bytes=64)
+        nc.vector.tensor_copy(
+            w2_codes[:].bitcast(U16).rearrange("p (a t m) -> p a t m", a=PASSES, t=PACK),
+            w2_raw[:].bitcast(U16).rearrange("p a (m t) -> p a t m", t=PACK),
+        )
+        w2_planes = keep.tile([P, PASSES * H], U8, name="w2_planes", align_bytes=64)
+        nc.vector.tensor_copy(
+            w2_planes[:].rearrange("p (a t m) -> p a t m", a=PASSES, t=PACK),
+            w2_planes_raw[:].rearrange("p (a m t) -> p a t m", a=PASSES, t=PACK),
+        )
+
+        w1_bf = keep.tile([P, PASSES, PACK * H], BF16, name="w1_bf", tag="w1_bf", align_bytes=64)
+        w1_mx = []
+        for a in range(PASSES):
+            round_and_deal(w1_bf[:, a, :], w1_raw[a][:])
+            w1_mx.append(quantise(w1_bf[:, a, :], f"w1_{a}"))
+        v_words.append(keep.tile([P, S], U32, name="v_words1", tag="w1_bf", align_bytes=64))
+
+        for c0 in range(0, S, BANK):
+            nc.vector.tensor_copy(v_words[1][:, c0 : c0 + BANK], tab[1][:].indirect(offsets(offs_sb, c0, BANK)))
+
+        w3_raw = keep.tile([P, PACK, N], F32, name="w3_raw", tag="big1", align_bytes=64)
+        nc.sync.dma_start(w3_raw[:], w3.rearrange("(p j) n -> p j n", j=PACK))
+
+        z_buf = keep.tile([P, DEPTH, BANK], F32, name="z_buf", tag="z")
+        turns_buf = keep.tile([P, DEPTH, BANK], I32, name="turns_buf", tag="turns", align_bytes=64)
+        r_buf = keep.tile([P, DEPTH, BANK], F32, name="r_buf", tag="r", align_bytes=64)
+        s_buf = keep.tile([P, DEPTH, BANK], F32, name="s_buf", tag="s")
+        th_buf = keep.tile([P, DEPTH, BANK], F32, name="th_buf", tag="th")
+        h = [keep.tile([P, S], F32, name=f"h{t}") for t in range(PACK)]
+        a1 = [keep.tile([P, PAIRS], F32, name=f"a1_{t}") for t in range(PACK)]
+        chunks = S // BANK
+        steps = PACK * chunks
+        piece = PAIRS // chunks
+
+        def reduce_angle(i):
+            t, c0 = i // chunks, (i % chunks) * BANK
+            cols = slice(c0, c0 + BANK)
+            e1 = psum.tile([P, BANK], F32, name="e1", tag="bank")
+            for a in range(PASSES):
+                codes, plane = w1_mx[a]
+                nc.tensor.matmul_mx(
+                    out=e1[:],
+                    lhsT=codes[:, t * P : (t + 1) * P].bitcast(FP8X4),
+                    lhsT_scale=plane[:, t * P : (t + 1) * P],
+                    rhs=v_words[a][:, cols].bitcast(FP8X4),
+                    rhs_scale=v_planes[a][:, cols],
+                    start=(a == 0),
+                    stop=(a == PASSES - 1),
+                )
+            z, turns, r = z_buf[:, i % DEPTH, :], turns_buf[:, i % DEPTH, :], r_buf[:, i % DEPTH, :]
+            nc.scalar.activation(z, e1[:], ACT.Abs, bias=-math.pi / 2)
+            if t == 0:
+                nc.vector.tensor_scalar(turns, z, 1 / (2 * math.pi), -0.25, ALU.mult, ALU.add)
+            else:
+                nc.scalar.activation(turns.bitcast(U32), z, ACT.Copy, scale=1 / (2 * math.pi), bias=-0.25)
+            nc.vector.scalar_tensor_tensor(r, turns, -2 * math.pi, z, ALU.mult, ALU.add)
+
+        def traits(i):
+            t, c0 = i // chunks, (i % chunks) * BANK
+            cols = slice(c0, c0 + BANK)
+            e2 = psum.tile([P, BANK], F32, name="e2", tag="bank")
+            for a in range(PASSES):
+                m0 = a * H + t * P
+                nc.tensor.matmul_mx(
+                    out=e2[:],
+                    lhsT=w2_codes[:, 2 * m0 : 2 * (m0 + P)].bitcast(FP4X4),
+                    lhsT_scale=w2_planes[:, m0 : m0 + P],
+                    rhs=v_words[a][:, cols].bitcast(FP8X4),
+                    rhs_scale=v_planes[a][:, cols],
+                    start=(a == 0),
+                    stop=(a == PASSES - 1),
+                )
+            r, s, th = r_buf[:, i % DEPTH, :], s_buf[:, i % DEPTH, :], th_buf[:, i % DEPTH, :]
+            nc.scalar.activation(s, r, ACT.Sin, scale=-1.0, bias=math.pi / 2)
+            nc.scalar.activation(th, e2[:], ACT.Tanh)
+            nc.vector.scalar_tensor_tensor(h[t][:, cols], s, gain_sb[:, t : t + 1], th, ALU.mult, ALU.mult)
+
+        def pair_piece(i):
+            t, m0 = i // chunks - 1, (i % chunks) * piece
+            second = th_buf[:, i % DEPTH, 0:piece]
+            nc.vector.tensor_copy(second, h[t][:].indirect(offsets(pos2_sb, m0, piece)))
+            nc.vector.tensor_tensor(
+                a1[t][:, m0 : m0 + piece], h[t][:].indirect(offsets(pos1_sb, m0, piece)), second, ALU.subtract
+            )
+
+        for i in range(steps + LAG):
+            if i < steps:
+                reduce_angle(i)
+            if i >= LAG:
+                traits(i - LAG)
+            if i - LAG >= chunks:
+                pair_piece(i - LAG)
+        last = PACK - 1
+        second = th_buf[:, 0:2, :].rearrange("p d c -> p (d c)")
+        nc.vector.tensor_copy(second, h[last][:].indirect(pos2_sb[:]))
+        nc.vector.tensor_tensor(a1[last][:], h[last][:].indirect(pos1_sb[:]), second, ALU.subtract)
+
+        w3_bf = keep.tile([P, GROUPS, PACK * 512], BF16, name="w3_bf", tag="turns", align_bytes=64)
+        for g in range(GROUPS):
+            round_and_deal(w3_bf[:, g, :], w3_raw[:, :, g * 512 : (g + 1) * 512])
+        w3_mx = [quantise(w3_bf[:, g, :], f"w3_{g}") for g in range(GROUPS)]
+
+        y = [keep.tile([P, PACK, KEPT], F32, name=f"y{g}", tag=f"big{g}", align_bytes=64) for g in range(GROUPS)]
+        y_codes = keep.tile([P, GROUPS, KEPT], U32, name="y_codes", align_bytes=64)
+        y_plane = keep.tile([P, GROUPS, KEPT], U8, name="y_plane", align_bytes=64)
+        out_rows = out_0.rearrange("(g p t) j -> g p t j", g=GROUPS, t=PACK)
+        out_words = out_1.rearrange("g p j i -> p g (j i)").bitcast(I32)
+        late = keep.tile([P, DEPTH, BANK], F32, name="late", tag="th")
+        suspect0 = late[:, 0:2, :].rearrange("p d (e c) -> p (d e) c", c=HALF)
+        kept = late[:, 2, :].rearrange("p (t c) -> p t c", t=PACK)
+        late2 = keep.tile([P, PACK, HALF], F32, name="late2", tag="r", align_bytes=64)
+        a2_woven0 = late2[:, 0, :].bitcast(BF16)
+        quarters = KEPT // OUT_COLS
+        made = {}
+
+        def pick_suspects(half, ts):
+            dst = suspect0 if half == 0 else late2
+            for t in ts:
+                nc.vector.tensor_copy(dst[:, t, :], h[t][:].indirect(offsets(pos4_sb, half * HALF, HALF)))
+
+        def pick_kept(q):
+            for t in range(PACK):
+                nc.vector.tensor_copy(kept[:, t, :], a1[t][:].indirect(offsets(pos3_sb, q * OUT_COLS, OUT_COLS)))
+
+        def larger(q):
+            src = suspect0 if q < 2 else late2
+            c0 = (q % 2) * OUT_COLS
+            a2 = ring.tile([P, PACK, OUT_COLS], BF16, name="a2")
+            nc.vector.tensor_tensor(a2[:], kept, src[:, :, c0 : c0 + OUT_COLS], ALU.max)
+            if q == 0:
+                woven = a2_woven0
+            else:
+                woven = ring.tile([P, OUT_COLS * PACK], BF16, name="a2_woven", align_bytes=64)[:]
+            nc.scalar.copy(woven.rearrange("p (j t) -> p j t", t=PACK), a2[:].rearrange("p t j -> p j t"))
+            made[q] = woven
+
+        def features(q):
+            cols = slice(q * OUT_COLS, (q + 1) * OUT_COLS)
+            a2_codes = ring.tile([P, OUT_COLS], U32, name="a2_codes", align_bytes=64)
+            a2_plane = ring.tile([P, OUT_COLS], U8, name="a2_plane", align_bytes=64)
+            nc.vector.quantize_mx(out=a2_codes[:].bitcast(FP8X4), scales=a2_plane[:], in_=made[q])
+            woven = []
+            for g in range(GROUPS):
+                acc = psum.tile([P, PACK, OUT_COLS], F32, name="acc", tag="bank")
+                codes, plane = w3_mx[g]
+                for t in range(PACK):
+                    nc.tensor.matmul_mx(
+                        out=acc[:, t, :],
+                        lhsT=codes[:, t * P : (t + 1) * P].bitcast(FP8X4),
+                        lhsT_scale=plane[:, t * P : (t + 1) * P],
+                        rhs=a2_codes[:].bitcast(FP8X4),
+                        rhs_scale=a2_plane[:],
+                        start=True,
+                        stop=True,
+                    )
+                copy = nc.vector.tensor_copy if (q == quarters - 1 and g == GROUPS - 1) else nc.scalar.copy
+                copy(y[g][:, :, cols], acc[:])
+                nc.sync.dma_start(out_rows[g][:, :, cols], y[g][:, :, cols])
+                y_woven = ring.tile([P, OUT_COLS * PACK], BF16, name="y_woven", align_bytes=64, bufs=4)
+                copy(y_woven[:].rearrange("p (j t) -> p j t", t=PACK), acc[:].rearrange("p t j -> p j t"))
+                woven.append(y_woven)
+            made[q] = woven
+
+        def planes(q):
+            cols = slice(q * OUT_COLS, (q + 1) * OUT_COLS)
+            for g in range(GROUPS):
+                nc.vector.quantize_mx(out=y_codes[:, g, cols].bitcast(FP8X4), scales=y_plane[:, g, cols], in_=made[q][g][:])
+            nc.sync.dma_start(out_words[:, :, cols], y_codes[:, :, cols].bitcast(I32))
+
+        pick_suspects(0, range(PACK))
+        pick_kept(0)
+        larger(0)
+        pick_kept(1)
+        features(0)
+        larger(1)
+        pick_suspects(1, range(PACK))
+        features(1)
+        planes(0)
+        pick_kept(2)
+        larger(2)
+        planes(1)
+        pick_kept(3)
+        features(2)
+        larger(3)
+        features(3)
+        planes(2)
+        planes(3)
+        for q in range(4):
+            nc.scalar.dma_start(
+                out_2[:, 4 * q : 4 * q + 4, :].rearrange("g r j -> r g j").bitcast(I32),
+                y_plane[32 * q : 32 * q + 4, :, :].bitcast(I32),
+            )

@@ -44,6 +44,11 @@ def tile_list_letter_stylometry_traits_kernel(
             nc.sync.dma_start(tile[:], src)
             return tile
 
+        warm_in = keep.tile([P, 1], F32, name="warm_in")
+        warm_out = keep.tile([P, 1], F32, name="warm_out")
+        nc.vector.memset(warm_in[:], 0.0)
+        nc.scalar.activation(warm_out[:], warm_in[:], ACT.Silu)
+
         scale_rows = keep.tile([P, T], U8, name="scale_rows", align_bytes=64)
         nc.vector.memset(scale_rows[32:64, :].bitcast(I32), 0)
         nc.vector.memset(scale_rows[64:128, :].bitcast(I32), 0)
@@ -51,13 +56,14 @@ def tile_list_letter_stylometry_traits_kernel(
         nc.gpsimd.memset(w2_planes_raw[:].bitcast(I32), 0)
         v_planes = [keep.tile([P, S], U8, name=f"v_plane{a}", align_bytes=64) for a in range(PASSES)]
         for a in range(PASSES):
-            nc.gpsimd.memset(v_planes[a][:].bitcast(I32), 0)
+            nc.vector.memset(v_planes[a][:].bitcast(I32), 0)
 
         offs_sb = load_list(offs, "offs_sb")
         nc.sync.dma_start(scale_rows[0:32, :].bitcast(I32), tab_scales.rearrange("a q t -> (a q) t").bitcast(I32))
-        tab = [keep.tile([P, T], U32, name=f"tab{a}", tag=f"big{a}", align_bytes=64) for a in range(PASSES)]
+        tab = []
 
         def load_tab(a):
+            tab.append(keep.tile([P, T], U32, name=f"tab{a}", tag=f"big{a}", align_bytes=64))
             nc.sync.dma_start(tab[a][:].bitcast(I32), tab_words[a].rearrange("p t i -> p (t i)").bitcast(I32))
 
         load_tab(0)
@@ -72,11 +78,11 @@ def tile_list_letter_stylometry_traits_kernel(
         nc.sync.dma_start(gain_sb[:], gain.rearrange("(p t) -> p t", t=PACK))
         pos1_sb = load_list(pos1, "pos1_sb")
         pos2_sb = load_list(pos2, "pos2_sb")
-        pos3_sb = load_list(pos3, "pos3_sb")
         w1_raw = [keep.tile([P, PACK, H], F32, name=f"w1_raw{a}", tag=f"raw{a}") for a in range(PASSES)]
         for a in range(PASSES):
             nc.sync.dma_start(w1_raw[a][:], w1[a * 512 : (a + 1) * 512, :].rearrange("(p j) c -> p j c", j=PACK))
         load_tab(1)
+        pos3_sb = load_list(pos3, "pos3_sb")
         pos4_sb = load_list(pos4, "pos4_sb")
 
         def offsets(tile, first, count):
@@ -84,9 +90,10 @@ def tile_list_letter_stylometry_traits_kernel(
 
         picked_rows = keep.tile([P, S], U8, name="picked_rows", align_bytes=64)
         nc.vector.tensor_copy(picked_rows[:], scale_rows[:].indirect(offs_sb[:]))
-        for a, queue in enumerate((nc.gpsimd, nc.scalar)):
+        for a in range(PASSES):
             for q in range(4):
                 row = 16 * a + 4 * q
+                queue = nc.scalar if a == 0 else nc.gpsimd
                 queue.dma_start(
                     v_planes[a][32 * q : 32 * q + 4, :].bitcast(I32), picked_rows[row : row + 4, :].bitcast(I32)
                 )

@@ -49,14 +49,19 @@ def tile_list_letter_stylometry_traits_kernel(
         nc.vector.memset(warm_in[:], 0.0)
         nc.scalar.activation(warm_out[:], warm_in[:], ACT.Silu)
 
-        scale_rows = keep.tile([P, T], U8, name="scale_rows", align_bytes=64)
+        scale_rows = keep.tile([P, T], U8, name="scale_rows", tag="big1", align_bytes=64)
         nc.vector.memset(scale_rows[32:64, :].bitcast(I32), 0)
         nc.vector.memset(scale_rows[64:128, :].bitcast(I32), 0)
         w2_planes_raw = keep.tile([P, PASSES * H], U8, name="w2_planes_raw", align_bytes=64)
         nc.gpsimd.memset(w2_planes_raw[:].bitcast(I32), 0)
+        for q in range(4):
+            nc.gpsimd.dma_start(
+                w2_planes_raw[32 * q : 32 * q + 4, :].rearrange("r (a c) -> r a c", a=PASSES).bitcast(I32),
+                w2_scales[:, 4 * q : 4 * q + 4, :].rearrange("a r c -> r a c").bitcast(I32),
+            )
         v_planes = [keep.tile([P, S], U8, name=f"v_plane{a}", align_bytes=64) for a in range(PASSES)]
         for a in range(PASSES):
-            nc.vector.memset(v_planes[a][:].bitcast(I32), 0)
+            nc.gpsimd.memset(v_planes[a][:].bitcast(I32), 0)
 
         offs_sb = load_list(offs, "offs_sb")
         nc.sync.dma_start(scale_rows[0:32, :].bitcast(I32), tab_scales.rearrange("a q t -> (a q) t").bitcast(I32))
@@ -67,21 +72,15 @@ def tile_list_letter_stylometry_traits_kernel(
             nc.sync.dma_start(tab[a][:].bitcast(I32), tab_words[a].rearrange("p t i -> p (t i)").bitcast(I32))
 
         load_tab(0)
-        w2_raw = keep.tile([P, PASSES, 2 * H], U8, name="w2_raw")
-        nc.sync.dma_start(w2_raw[:].bitcast(I32), w2_words.rearrange("a p c -> p a c").bitcast(I32))
-        for q in range(4):
-            nc.gpsimd.dma_start(
-                w2_planes_raw[32 * q : 32 * q + 4, :].rearrange("r (a c) -> r a c", a=PASSES).bitcast(I32),
-                w2_scales[:, 4 * q : 4 * q + 4, :].rearrange("a r c -> r a c").bitcast(I32),
-            )
-        gain_sb = keep.tile([P, PACK], F32, name="gain_sb")
-        nc.sync.dma_start(gain_sb[:], gain.rearrange("(p t) -> p t", t=PACK))
         pos1_sb = load_list(pos1, "pos1_sb")
         pos2_sb = load_list(pos2, "pos2_sb")
-        w1_raw = [keep.tile([P, PACK, H], F32, name=f"w1_raw{a}", tag=f"raw{a}") for a in range(PASSES)]
+        gain_sb = keep.tile([P, PACK], F32, name="gain_sb")
+        nc.sync.dma_start(gain_sb[:], gain.rearrange("(p t) -> p t", t=PACK))
+        w1_raw = [keep.tile([P, PACK, H], F32, name=f"w1_raw{a}") for a in range(PASSES)]
         for a in range(PASSES):
             nc.sync.dma_start(w1_raw[a][:], w1[a * 512 : (a + 1) * 512, :].rearrange("(p j) c -> p j c", j=PACK))
-        load_tab(1)
+        w2_raw = keep.tile([P, PASSES, 2 * H], U8, name="w2_raw")
+        nc.sync.dma_start(w2_raw[:].bitcast(I32), w2_words.rearrange("a p c -> p a c").bitcast(I32))
         pos3_sb = load_list(pos3, "pos3_sb")
         pos4_sb = load_list(pos4, "pos4_sb")
 
@@ -93,10 +92,11 @@ def tile_list_letter_stylometry_traits_kernel(
         for a in range(PASSES):
             for q in range(4):
                 row = 16 * a + 4 * q
-                queue = nc.scalar if a == 0 else nc.gpsimd
-                queue.dma_start(
+                nc.sync.dma_start(
                     v_planes[a][32 * q : 32 * q + 4, :].bitcast(I32), picked_rows[row : row + 4, :].bitcast(I32)
                 )
+                if row == 0:
+                    load_tab(1)
         v_words = [keep.tile([P, S], U32, name="v_words0", align_bytes=64)]
         nc.vector.tensor_copy(v_words[0][:], tab[0][:].indirect(offs_sb[:]))
 
@@ -186,29 +186,35 @@ def tile_list_letter_stylometry_traits_kernel(
                     stop=(a == PASSES - 1),
                 )
             r, s, th = r_buf[:, i % DEPTH, :], s_buf[:, i % DEPTH, :], th_buf[:, i % DEPTH, :]
-            nc.scalar.activation(s, r, ACT.Sin, scale=-1.0, bias=math.pi / 2)
             nc.scalar.activation(th, e2[:], ACT.Tanh)
+            nc.scalar.activation(s, r, ACT.Sin, scale=-1.0, bias=math.pi / 2)
+            if t > 0:
+                pick_second(t - 1, (i % chunks) * piece, piece, r[:, 0:piece])
             nc.vector.scalar_tensor_tensor(h[t][:, cols], s, gain_sb[:, t : t + 1], th, ALU.mult, ALU.mult)
+            if t > 0:
+                subtract_from_first(t - 1, (i % chunks) * piece, piece, r[:, 0:piece])
+            if i % chunks == chunks - 1:
+                nc.vector.tensor_copy(suspect0[:, t, :], h[t][:].indirect(offsets(pos4_sb, 0, HALF)))
 
-        def pair_piece(i):
-            t, m0 = i // chunks - 1, (i % chunks) * piece
-            second = th_buf[:, i % DEPTH, 0:piece]
-            nc.vector.tensor_copy(second, h[t][:].indirect(offsets(pos2_sb, m0, piece)))
+        def pick_second(t, m0, count, second):
+            nc.vector.tensor_copy(second, h[t][:].indirect(offsets(pos2_sb, m0, count)))
+
+        def subtract_from_first(t, m0, count, second):
             nc.vector.tensor_tensor(
-                a1[t][:, m0 : m0 + piece], h[t][:].indirect(offsets(pos1_sb, m0, piece)), second, ALU.subtract
+                a1[t][:, m0 : m0 + count], h[t][:].indirect(offsets(pos1_sb, m0, count)), second, ALU.subtract
             )
 
+        suspect0 = keep.tile([P, PACK, HALF], F32, name="suspect0")
         for i in range(steps + LAG):
             if i < steps:
                 reduce_angle(i)
             if i >= LAG:
                 traits(i - LAG)
-            if i - LAG >= chunks:
-                pair_piece(i - LAG)
         last = PACK - 1
-        second = th_buf[:, 0:2, :].rearrange("p d c -> p (d c)")
-        nc.vector.tensor_copy(second, h[last][:].indirect(pos2_sb[:]))
-        nc.vector.tensor_tensor(a1[last][:], h[last][:].indirect(pos1_sb[:]), second, ALU.subtract)
+        for half in range(2):
+            pick_second(last, half * BANK, BANK, r_buf[:, half, :])
+        for half in range(2):
+            subtract_from_first(last, half * BANK, BANK, r_buf[:, half, :])
 
         w3_bf = keep.tile([P, GROUPS, PACK * 512], BF16, name="w3_bf", tag="turns", align_bytes=64)
         for g in range(GROUPS):
@@ -220,34 +226,30 @@ def tile_list_letter_stylometry_traits_kernel(
         y_plane = keep.tile([P, GROUPS, KEPT], U8, name="y_plane", align_bytes=64)
         out_rows = out_0.rearrange("(g p t) j -> g p t j", g=GROUPS, t=PACK)
         out_words = out_1.rearrange("g p j i -> p g (j i)").bitcast(I32)
-        late = keep.tile([P, DEPTH, BANK], F32, name="late", tag="th")
-        suspect0 = late[:, 0:2, :].rearrange("p d (e c) -> p (d e) c", c=HALF)
-        kept = late[:, 2, :].rearrange("p (t c) -> p t c", t=PACK)
-        late2 = keep.tile([P, PACK, HALF], F32, name="late2", tag="r", align_bytes=64)
-        a2_woven0 = late2[:, 0, :].bitcast(BF16)
+        kept = keep.tile([P, 2, PACK, OUT_COLS], F32, name="kept", tag="th")
+        suspect1 = keep.tile([P, PACK, HALF], F32, name="suspect1", tag="s")
         quarters = KEPT // OUT_COLS
         made = {}
 
-        def pick_suspects(half, ts):
-            dst = suspect0 if half == 0 else late2
-            for t in ts:
-                nc.vector.tensor_copy(dst[:, t, :], h[t][:].indirect(offsets(pos4_sb, half * HALF, HALF)))
+        def pick_suspects():
+            for t in range(PACK):
+                nc.vector.tensor_copy(suspect1[:, t, :], h[t][:].indirect(offsets(pos4_sb, HALF, HALF)))
 
         def pick_kept(q):
             for t in range(PACK):
-                nc.vector.tensor_copy(kept[:, t, :], a1[t][:].indirect(offsets(pos3_sb, q * OUT_COLS, OUT_COLS)))
+                nc.vector.tensor_copy(kept[:, q % 2, t, :], a1[t][:].indirect(offsets(pos3_sb, q * OUT_COLS, OUT_COLS)))
 
         def larger(q):
-            src = suspect0 if q < 2 else late2
+            src = suspect0 if q < 2 else suspect1
             c0 = (q % 2) * OUT_COLS
-            a2 = ring.tile([P, PACK, OUT_COLS], BF16, name="a2")
-            nc.vector.tensor_tensor(a2[:], kept, src[:, :, c0 : c0 + OUT_COLS], ALU.max)
             if q == 0:
-                woven = a2_woven0
+                a2 = suspect1[:].bitcast(BF16)[:, :, 0:OUT_COLS]
             else:
-                woven = ring.tile([P, OUT_COLS * PACK], BF16, name="a2_woven", align_bytes=64)[:]
-            nc.scalar.copy(woven.rearrange("p (j t) -> p j t", t=PACK), a2[:].rearrange("p t j -> p j t"))
-            made[q] = woven
+                a2 = ring.tile([P, PACK, OUT_COLS], BF16, name="a2")[:]
+            nc.vector.tensor_tensor(a2, kept[:, q % 2], src[:, :, c0 : c0 + OUT_COLS], ALU.max)
+            woven = ring.tile([P, OUT_COLS * PACK], BF16, name="a2_woven", align_bytes=64)
+            nc.scalar.copy(woven[:].rearrange("p (j t) -> p j t", t=PACK), a2.rearrange("p t j -> p j t"))
+            made[q] = woven[:]
 
         def features(q):
             cols = slice(q * OUT_COLS, (q + 1) * OUT_COLS)
@@ -282,13 +284,12 @@ def tile_list_letter_stylometry_traits_kernel(
                 nc.vector.quantize_mx(out=y_codes[:, g, cols].bitcast(FP8X4), scales=y_plane[:, g, cols], in_=made[q][g][:])
             nc.sync.dma_start(out_words[:, :, cols], y_codes[:, :, cols].bitcast(I32))
 
-        pick_suspects(0, range(PACK))
         pick_kept(0)
         larger(0)
         pick_kept(1)
         features(0)
         larger(1)
-        pick_suspects(1, range(PACK))
+        pick_suspects()
         features(1)
         planes(0)
         pick_kept(2)

@@ -26,7 +26,7 @@ PER_COL = 16
 OUT_COLS = 128
 HALF = 256
 DEPTH = 4
-LAG = 2
+LAG = 1
 
 
 def tile_list_letter_stylometry_traits_kernel(
@@ -49,7 +49,7 @@ def tile_list_letter_stylometry_traits_kernel(
         nc.vector.memset(warm_in[:], 0.0)
         nc.scalar.activation(warm_out[:], warm_in[:], ACT.Silu)
 
-        scale_rows = keep.tile([P, T], U8, name="scale_rows", tag="big1", align_bytes=64)
+        scale_rows = keep.tile([P, T], U8, name="scale_rows", align_bytes=64)
         nc.vector.memset(scale_rows[32:64, :].bitcast(I32), 0)
         nc.vector.memset(scale_rows[64:128, :].bitcast(I32), 0)
         w2_planes_raw = keep.tile([P, PASSES * H], U8, name="w2_planes_raw", align_bytes=64)
@@ -63,24 +63,24 @@ def tile_list_letter_stylometry_traits_kernel(
         for a in range(PASSES):
             nc.gpsimd.memset(v_planes[a][:].bitcast(I32), 0)
 
-        offs_sb = load_list(offs, "offs_sb")
         nc.sync.dma_start(scale_rows[0:32, :].bitcast(I32), tab_scales.rearrange("a q t -> (a q) t").bitcast(I32))
-        tab = []
+        offs_sb = load_list(offs, "offs_sb")
+        tab = [keep.tile([P, T], U32, name=f"tab{a}", tag=f"big{a}", align_bytes=64) for a in range(PASSES)]
 
         def load_tab(a):
-            tab.append(keep.tile([P, T], U32, name=f"tab{a}", tag=f"big{a}", align_bytes=64))
             nc.sync.dma_start(tab[a][:].bitcast(I32), tab_words[a].rearrange("p t i -> p (t i)").bitcast(I32))
 
         load_tab(0)
-        pos1_sb = load_list(pos1, "pos1_sb")
-        pos2_sb = load_list(pos2, "pos2_sb")
-        gain_sb = keep.tile([P, PACK], F32, name="gain_sb")
-        nc.sync.dma_start(gain_sb[:], gain.rearrange("(p t) -> p t", t=PACK))
         w1_raw = [keep.tile([P, PACK, H], F32, name=f"w1_raw{a}") for a in range(PASSES)]
         for a in range(PASSES):
             nc.sync.dma_start(w1_raw[a][:], w1[a * 512 : (a + 1) * 512, :].rearrange("(p j) c -> p j c", j=PACK))
         w2_raw = keep.tile([P, PASSES, 2 * H], U8, name="w2_raw")
         nc.sync.dma_start(w2_raw[:].bitcast(I32), w2_words.rearrange("a p c -> p a c").bitcast(I32))
+        load_tab(1)
+        gain_sb = keep.tile([P, PACK], F32, name="gain_sb")
+        nc.sync.dma_start(gain_sb[:], gain.rearrange("(p t) -> p t", t=PACK))
+        pos1_sb = load_list(pos1, "pos1_sb")
+        pos2_sb = load_list(pos2, "pos2_sb")
         pos3_sb = load_list(pos3, "pos3_sb")
         pos4_sb = load_list(pos4, "pos4_sb")
 
@@ -95,8 +95,6 @@ def tile_list_letter_stylometry_traits_kernel(
                 nc.sync.dma_start(
                     v_planes[a][32 * q : 32 * q + 4, :].bitcast(I32), picked_rows[row : row + 4, :].bitcast(I32)
                 )
-                if row == 0:
-                    load_tab(1)
         v_words = [keep.tile([P, S], U32, name="v_words0", align_bytes=64)]
         nc.vector.tensor_copy(v_words[0][:], tab[0][:].indirect(offs_sb[:]))
 
@@ -140,7 +138,7 @@ def tile_list_letter_stylometry_traits_kernel(
         turns_buf = keep.tile([P, DEPTH, BANK], I32, name="turns_buf", tag="turns", align_bytes=64)
         r_buf = keep.tile([P, DEPTH, BANK], F32, name="r_buf", tag="r", align_bytes=64)
         s_buf = keep.tile([P, DEPTH, BANK], F32, name="s_buf", tag="s")
-        th_buf = keep.tile([P, DEPTH, BANK], F32, name="th_buf", tag="th")
+        th_buf = keep.tile([P, DEPTH, BANK], F32, name="th_buf", tag="th", align_bytes=64)
         h = [keep.tile([P, S], F32, name=f"h{t}") for t in range(PACK)]
         a1 = [keep.tile([P, PAIRS], F32, name=f"a1_{t}") for t in range(PACK)]
         chunks = S // BANK
@@ -164,7 +162,7 @@ def tile_list_letter_stylometry_traits_kernel(
                 )
             z, turns, r = z_buf[:, i % DEPTH, :], turns_buf[:, i % DEPTH, :], r_buf[:, i % DEPTH, :]
             nc.scalar.activation(z, e1[:], ACT.Abs, bias=-math.pi / 2)
-            if t == 0:
+            if i <= chunks:
                 nc.vector.tensor_scalar(turns, z, 1 / (2 * math.pi), -0.25, ALU.mult, ALU.add)
             else:
                 nc.scalar.activation(turns.bitcast(U32), z, ACT.Copy, scale=1 / (2 * math.pi), bias=-0.25)
@@ -222,11 +220,10 @@ def tile_list_letter_stylometry_traits_kernel(
         w3_mx = [quantise(w3_bf[:, g, :], f"w3_{g}") for g in range(GROUPS)]
 
         y = [keep.tile([P, PACK, KEPT], F32, name=f"y{g}", tag=f"big{g}", align_bytes=64) for g in range(GROUPS)]
-        y_codes = keep.tile([P, GROUPS, KEPT], U32, name="y_codes", align_bytes=64)
         y_plane = keep.tile([P, GROUPS, KEPT], U8, name="y_plane", align_bytes=64)
         out_rows = out_0.rearrange("(g p t) j -> g p t j", g=GROUPS, t=PACK)
         out_words = out_1.rearrange("g p j i -> p g (j i)").bitcast(I32)
-        kept = keep.tile([P, 2, PACK, OUT_COLS], F32, name="kept", tag="th")
+        kept = keep.tile([P, 2, PACK, OUT_COLS], F32, name="kept", tag="th", align_bytes=64)
         suspect1 = keep.tile([P, PACK, HALF], F32, name="suspect1", tag="s")
         quarters = KEPT // OUT_COLS
         made = {}
@@ -273,7 +270,7 @@ def tile_list_letter_stylometry_traits_kernel(
                 copy = nc.vector.tensor_copy if (q == quarters - 1 and g == GROUPS - 1) else nc.scalar.copy
                 copy(y[g][:, :, cols], acc[:])
                 nc.sync.dma_start(out_rows[g][:, :, cols], y[g][:, :, cols])
-                y_woven = ring.tile([P, OUT_COLS * PACK], BF16, name="y_woven", align_bytes=64, bufs=4)
+                y_woven = ring.tile([P, OUT_COLS * PACK], BF16, name="y_woven", align_bytes=64, bufs=8)
                 copy(y_woven[:].rearrange("p (j t) -> p j t", t=PACK), acc[:].rearrange("p t j -> p j t"))
                 woven.append(y_woven)
             made[q] = woven
@@ -282,7 +279,6 @@ def tile_list_letter_stylometry_traits_kernel(
             cols = slice(q * OUT_COLS, (q + 1) * OUT_COLS)
             for g in range(GROUPS):
                 nc.vector.quantize_mx(out=y_codes[:, g, cols].bitcast(FP8X4), scales=y_plane[:, g, cols], in_=made[q][g][:])
-            nc.sync.dma_start(out_words[:, :, cols], y_codes[:, :, cols].bitcast(I32))
 
         pick_kept(0)
         larger(0)
@@ -291,16 +287,20 @@ def tile_list_letter_stylometry_traits_kernel(
         larger(1)
         pick_suspects()
         features(1)
-        planes(0)
         pick_kept(2)
         larger(2)
-        planes(1)
         pick_kept(3)
         features(2)
         larger(3)
         features(3)
-        planes(2)
-        planes(3)
+        y_codes = keep.tile([P, GROUPS, KEPT], U32, name="y_codes", tag="th", align_bytes=64)
+        for q in range(quarters - 1):
+            planes(q)
+        early = slice(0, KEPT - OUT_COLS)
+        nc.sync.dma_start(out_words[:, :, early], y_codes[:, :, early].bitcast(I32))
+        planes(quarters - 1)
+        late = slice(KEPT - OUT_COLS, KEPT)
+        nc.sync.dma_start(out_words[:, :, late], y_codes[:, :, late].bitcast(I32))
         for q in range(4):
             nc.scalar.dma_start(
                 out_2[:, 4 * q : 4 * q + 4, :].rearrange("g r j -> r g j").bitcast(I32),

import math
from contextlib import ExitStack

import concourse.mybir as mybir

K, T, S, PAIRS, KEPT, H, N = 1024, 4096, 2048, 1024, 512, 512, 1024
FLOPS = 2 * K * H * S * 2 + 2 * H * N * KEPT

F32 = mybir.dt.float32
BF16 = mybir.dt.bfloat16
I32 = mybir.dt.int32
U32 = mybir.dt.uint32
U16 = mybir.dt.uint16
U8 = mybir.dt.uint8
FP8X4 = mybir.dt.float8_e4m3fn_x4
FP4X4 = mybir.dt.float4_e2m1fn_x4
ALU = mybir.AluOpType
ACT = mybir.ActivationFunctionType

P = 128
PACK = 4
PASSES = K // (P * PACK)
GROUPS = N // (P * PACK)
BANK = 512
PER_COL = 16
OUT_COLS = 128
HALF = 256
DEPTH = 4
LAG = 1


def tile_list_letter_stylometry_traits_kernel(
    tc, tab_words, tab_scales, offs, w1, w2_words, w2_scales, gain, pos1, pos2, pos3, pos4, w3, out_0, out_1, out_2
):
    nc = tc.nc
    with ExitStack() as ctx:
        lists = ctx.enter_context(tc.tile_pool(name="lists", bufs=1))
        keep = ctx.enter_context(tc.tile_pool(name="keep", bufs=1))
        ring = ctx.enter_context(tc.tile_pool(name="ring", bufs=2))
        psum = ctx.enter_context(tc.psum_pool(name="psum", bufs=8))

        def load_list(src, name):
            tile = lists.tile(list(src.shape), U16, name=name)
            nc.sync.dma_start(tile[:], src)
            return tile

        warm_in = keep.tile([P, 1], F32, name="warm_in")
        warm_out = keep.tile([P, 1], F32, name="warm_out")
        nc.vector.memset(warm_in[:], 0.0)
        nc.scalar.activation(warm_out[:], warm_in[:], ACT.Silu)

        scale_rows = keep.tile([P, T], U8, name="scale_rows", align_bytes=64)
        nc.vector.memset(scale_rows[32:64, :].bitcast(I32), 0)
        nc.vector.memset(scale_rows[64:128, :].bitcast(I32), 0)
        w2_planes_raw = keep.tile([P, PASSES * H], U8, name="w2_planes_raw", align_bytes=64)
        nc.gpsimd.memset(w2_planes_raw[:].bitcast(I32), 0)
        for q in range(4):
            nc.gpsimd.dma_start(
                w2_planes_raw[32 * q : 32 * q + 4, :].rearrange("r (a c) -> r a c", a=PASSES).bitcast(I32),
                w2_scales[:, 4 * q : 4 * q + 4, :].rearrange("a r c -> r a c").bitcast(I32),
            )
        v_planes = [keep.tile([P, S], U8, name=f"v_plane{a}", align_bytes=64) for a in range(PASSES)]
        for a in range(PASSES):
            nc.gpsimd.memset(v_planes[a][:].bitcast(I32), 0)

        nc.sync.dma_start(scale_rows[0:32, :].bitcast(I32), tab_scales.rearrange("a q t -> (a q) t").bitcast(I32))
        offs_sb = load_list(offs, "offs_sb")
        tab = [keep.tile([P, T], U32, name=f"tab{a}", tag=f"big{a}", align_bytes=64) for a in range(PASSES)]

        def load_tab(a):
            nc.sync.dma_start(tab[a][:].bitcast(I32), tab_words[a].rearrange("p t i -> p (t i)").bitcast(I32))

        load_tab(0)
        w1_raw = [keep.tile([P, PACK, H], F32, name=f"w1_raw{a}") for a in range(PASSES)]
        for a in range(PASSES):
            nc.sync.dma_start(w1_raw[a][:], w1[a * 512 : (a + 1) * 512, :].rearrange("(p j) c -> p j c", j=PACK))
        w2_raw = keep.tile([P, PASSES, 2 * H], U8, name="w2_raw")
        nc.sync.dma_start(w2_raw[:].bitcast(I32), w2_words.rearrange("a p c -> p a c").bitcast(I32))
        load_tab(1)
        gain_sb = keep.tile([P, PACK], F32, name="gain_sb")
        nc.sync.dma_start(gain_sb[:], gain.rearrange("(p t) -> p t", t=PACK))
        pos1_sb = load_list(pos1, "pos1_sb")
        pos2_sb = load_list(pos2, "pos2_sb")
        pos3_sb = load_list(pos3, "pos3_sb")
        pos4_sb = load_list(pos4, "pos4_sb")

        def offsets(tile, first, count):
            return tile[:, first // PER_COL : (first + count) // PER_COL]

        picked_rows = keep.tile([P, S], U8, name="picked_rows", align_bytes=64)
        nc.vector.tensor_copy(picked_rows[:], scale_rows[:].indirect(offs_sb[:]))
        for a in range(PASSES):
            for q in range(4):
                row = 16 * a + 4 * q
                nc.sync.dma_start(
                    v_planes[a][32 * q : 32 * q + 4, :].bitcast(I32), picked_rows[row : row + 4, :].bitcast(I32)
                )
        v_words = [keep.tile([P, S], U32, name="v_words0", align_bytes=64)]
        nc.vector.tensor_copy(v_words[0][:], tab[0][:].indirect(offs_sb[:]))

        def round_and_deal(dealt, raw):
            nc.scalar.copy(
                dealt.rearrange("p (t m j) -> p m t j", t=PACK, j=PACK),
                raw.rearrange("p j (m t) -> p m t j", t=PACK),
            )

        def quantise(rounded, name):
            codes = keep.tile([P, 512], U32, name=name + "_codes", align_bytes=64)
            plane = keep.tile([P, 512], U8, name=name + "_plane", align_bytes=64)
            nc.vector.quantize_mx(out=codes[:].bitcast(FP8X4), scales=plane[:], in_=rounded)
            return codes, plane

        w2_codes = keep.tile([P, PASSES * 2 * H], U8, name="w2_codes", align_bytes=64)
        nc.vector.tensor_copy(
            w2_codes[:].bitcast(U16).rearrange("p (a t m) -> p a t m", a=PASSES, t=PACK),
            w2_raw[:].bitcast(U16).rearrange("p a (m t) -> p a t m", t=PACK),
        )
        w2_planes = keep.tile([P, PASSES * H], U8, name="w2_planes", align_bytes=64)
        nc.vector.tensor_copy(
            w2_planes[:].rearrange("p (a t m) -> p a t m", a=PASSES, t=PACK),
            w2_planes_raw[:].rearrange("p (a m t) -> p a t m", a=PASSES, t=PACK),
        )

        w1_bf = keep.tile([P, PASSES, PACK * H], BF16, name="w1_bf", tag="w1_bf", align_bytes=64)
        w1_mx = []
        for a in range(PASSES):
            round_and_deal(w1_bf[:, a, :], w1_raw[a][:])
            w1_mx.append(quantise(w1_bf[:, a, :], f"w1_{a}"))
        v_words.append(keep.tile([P, S], U32, name="v_words1", tag="w1_bf", align_bytes=64))

        for c0 in range(0, S, BANK):
            nc.vector.tensor_copy(v_words[1][:, c0 : c0 + BANK], tab[1][:].indirect(offsets(offs_sb, c0, BANK)))

        w3_raw = keep.tile([P, PACK, N], F32, name="w3_raw", tag="big1", align_bytes=64)
        nc.sync.dma_start(w3_raw[:], w3.rearrange("(p j) n -> p j n", j=PACK))

        z_buf = keep.tile([P, DEPTH, BANK], F32, name="z_buf", tag="z")
        turns_buf = keep.tile([P, DEPTH, BANK], I32, name="turns_buf", tag="turns", align_bytes=64)
        r_buf = keep.tile([P, DEPTH, BANK], F32, name="r_buf", tag="r", align_bytes=64)
        s_buf = keep.tile([P, DEPTH, BANK], F32, name="s_buf", tag="s")
        th_buf = keep.tile([P, DEPTH, BANK], F32, name="th_buf", tag="th", align_bytes=64)
        h = [keep.tile([P, S], F32, name=f"h{t}") for t in range(PACK)]
        a1 = [keep.tile([P, PAIRS], F32, name=f"a1_{t}") for t in range(PACK)]
        chunks = S // BANK
        steps = PACK * chunks
        piece = PAIRS // chunks

        def reduce_angle(i):
            t, c0 = i // chunks, (i % chunks) * BANK
            cols = slice(c0, c0 + BANK)
            e1 = psum.tile([P, BANK], F32, name="e1", tag="bank")
            for a in range(PASSES):
                codes, plane = w1_mx[a]
                nc.tensor.matmul_mx(
                    out=e1[:],
                    lhsT=codes[:, t * P : (t + 1) * P].bitcast(FP8X4),
                    lhsT_scale=plane[:, t * P : (t + 1) * P],
                    rhs=v_words[a][:, cols].bitcast(FP8X4),
                    rhs_scale=v_planes[a][:, cols],
                    start=(a == 0),
                    stop=(a == PASSES - 1),
                )
            z, turns, r = z_buf[:, i % DEPTH, :], turns_buf[:, i % DEPTH, :], r_buf[:, i % DEPTH, :]
            nc.scalar.activation(z, e1[:], ACT.Abs, bias=-math.pi / 2)
            if i <= chunks:
                nc.vector.tensor_scalar(turns, z, 1 / (2 * math.pi), -0.25, ALU.mult, ALU.add)
            else:
                nc.scalar.activation(turns.bitcast(U32), z, ACT.Copy, scale=1 / (2 * math.pi), bias=-0.25)
            nc.vector.scalar_tensor_tensor(r, turns, -2 * math.pi, z, ALU.mult, ALU.add)

        def traits(i):
            t, c0 = i // chunks, (i % chunks) * BANK
            cols = slice(c0, c0 + BANK)
            e2 = psum.tile([P, BANK], F32, name="e2", tag="bank")
            for a in range(PASSES):
                m0 = a * H + t * P
                nc.tensor.matmul_mx(
                    out=e2[:],
                    lhsT=w2_codes[:, 2 * m0 : 2 * (m0 + P)].bitcast(FP4X4),
                    lhsT_scale=w2_planes[:, m0 : m0 + P],
                    rhs=v_words[a][:, cols].bitcast(FP8X4),
                    rhs_scale=v_planes[a][:, cols],
                    start=(a == 0),
                    stop=(a == PASSES - 1),
                )
            r, s, th = r_buf[:, i % DEPTH, :], s_buf[:, i % DEPTH, :], th_buf[:, i % DEPTH, :]
            nc.scalar.activation(th, e2[:], ACT.Tanh)
            nc.scalar.activation(s, r, ACT.Sin, scale=-1.0, bias=math.pi / 2)
            if t > 0:
                pick_second(t - 1, (i % chunks) * piece, piece, r[:, 0:piece])
            nc.vector.scalar_tensor_tensor(h[t][:, cols], s, gain_sb[:, t : t + 1], th, ALU.mult, ALU.mult)
            if t > 0:
                subtract_from_first(t - 1, (i % chunks) * piece, piece, r[:, 0:piece])
            if i % chunks == chunks - 1:
                nc.vector.tensor_copy(suspect0[:, t, :], h[t][:].indirect(offsets(pos4_sb, 0, HALF)))

        def pick_second(t, m0, count, second):
            nc.vector.tensor_copy(second, h[t][:].indirect(offsets(pos2_sb, m0, count)))

        def subtract_from_first(t, m0, count, second):
            nc.vector.tensor_tensor(
                a1[t][:, m0 : m0 + count], h[t][:].indirect(offsets(pos1_sb, m0, count)), second, ALU.subtract
            )

        suspect0 = keep.tile([P, PACK, HALF], F32, name="suspect0")
        for i in range(steps + LAG):
            if i < steps:
                reduce_angle(i)
            if i >= LAG:
                traits(i - LAG)
        last = PACK - 1
        for half in range(2):
            pick_second(last, half * BANK, BANK, r_buf[:, half, :])
        for half in range(2):
            subtract_from_first(last, half * BANK, BANK, r_buf[:, half, :])

        w3_bf = keep.tile([P, GROUPS, PACK * 512], BF16, name="w3_bf", tag="turns", align_bytes=64)
        for g in range(GROUPS):
            round_and_deal(w3_bf[:, g, :], w3_raw[:, :, g * 512 : (g + 1) * 512])
        w3_mx = [quantise(w3_bf[:, g, :], f"w3_{g}") for g in range(GROUPS)]

        y = [keep.tile([P, PACK, KEPT], F32, name=f"y{g}", tag=f"big{g}", align_bytes=64) for g in range(GROUPS)]
        y_plane = keep.tile([P, GROUPS, KEPT], U8, name="y_plane", align_bytes=64)
        out_rows = out_0.rearrange("(g p t) j -> g p t j", g=GROUPS, t=PACK)
        out_words = out_1.rearrange("g p j i -> p g (j i)").bitcast(I32)
        kept = keep.tile([P, 2, PACK, OUT_COLS], F32, name="kept", tag="th", align_bytes=64)
        suspect1 = keep.tile([P, PACK, HALF], F32, name="suspect1", tag="s")
        quarters = KEPT // OUT_COLS
        made = {}

        def pick_suspects():
            for t in range(PACK):
                nc.vector.tensor_copy(suspect1[:, t, :], h[t][:].indirect(offsets(pos4_sb, HALF, HALF)))

        def pick_kept(q):
            for t in range(PACK):
                nc.vector.tensor_copy(kept[:, q % 2, t, :], a1[t][:].indirect(offsets(pos3_sb, q * OUT_COLS, OUT_COLS)))

        def larger(q):
            src = suspect0 if q < 2 else suspect1
            c0 = (q % 2) * OUT_COLS
            if q == 0:
                a2 = suspect1[:].bitcast(BF16)[:, :, 0:OUT_COLS]
            else:
                a2 = ring.tile([P, PACK, OUT_COLS], BF16, name="a2")[:]
            nc.vector.tensor_tensor(a2, kept[:, q % 2], src[:, :, c0 : c0 + OUT_COLS], ALU.max)
            woven = ring.tile([P, OUT_COLS * PACK], BF16, name="a2_woven", align_bytes=64)
            nc.scalar.copy(woven[:].rearrange("p (j t) -> p j t", t=PACK), a2.rearrange("p t j -> p j t"))
            made[q] = woven[:]

        def features(q):
            cols = slice(q * OUT_COLS, (q + 1) * OUT_COLS)
            a2_codes = ring.tile([P, OUT_COLS], U32, name="a2_codes", align_bytes=64)
            a2_plane = ring.tile([P, OUT_COLS], U8, name="a2_plane", align_bytes=64)
            nc.vector.quantize_mx(out=a2_codes[:].bitcast(FP8X4), scales=a2_plane[:], in_=made[q])
            woven = []
            for g in range(GROUPS):
                acc = psum.tile([P, PACK, OUT_COLS], F32, name="acc", tag="bank")
                codes, plane = w3_mx[g]
                for t in range(PACK):
                    nc.tensor.matmul_mx(
                        out=acc[:, t, :],
                        lhsT=codes[:, t * P : (t + 1) * P].bitcast(FP8X4),
                        lhsT_scale=plane[:, t * P : (t + 1) * P],
                        rhs=a2_codes[:].bitcast(FP8X4),
                        rhs_scale=a2_plane[:],
                        start=True,
                        stop=True,
                    )
                copy = nc.vector.tensor_copy if (q == quarters - 1 and g == GROUPS - 1) else nc.scalar.copy
                copy(y[g][:, :, cols], acc[:])
                nc.sync.dma_start(out_rows[g][:, :, cols], y[g][:, :, cols])
                y_woven = ring.tile([P, OUT_COLS * PACK], BF16, name="y_woven", align_bytes=64, bufs=8)
                copy(y_woven[:].rearrange("p (j t) -> p j t", t=PACK), acc[:].rearrange("p t j -> p j t"))
                woven.append(y_woven)
            made[q] = woven

        def planes(q):
            cols = slice(q * OUT_COLS, (q + 1) * OUT_COLS)
            for g in range(GROUPS):
                nc.vector.quantize_mx(out=y_codes[:, g, cols].bitcast(FP8X4), scales=y_plane[:, g, cols], in_=made[q][g][:])

        pick_kept(0)
        larger(0)
        pick_kept(1)
        features(0)
        larger(1)
        pick_suspects()
        features(1)
        pick_kept(2)
        larger(2)
        pick_kept(3)
        features(2)
        larger(3)
        features(3)
        y_codes = keep.tile([P, GROUPS, KEPT], U32, name="y_codes", tag="th", align_bytes=64)
        for q in range(quarters - 1):
            planes(q)
        early = slice(0, KEPT - OUT_COLS)
        nc.sync.dma_start(out_words[:, :, early], y_codes[:, :, early].bitcast(I32))
        planes(quarters - 1)
        late = slice(KEPT - OUT_COLS, KEPT)
        nc.sync.dma_start(out_words[:, :, late], y_codes[:, :, late].bitcast(I32))
        for q in range(4):
            nc.scalar.dma_start(
                out_2[:, 4 * q : 4 * q + 4, :].rearrange("g r j -> r g j").bitcast(I32),
                y_plane[32 * q : 32 * q + 4, :, :].bitcast(I32),
            )
